import numpy as np
import ml_dtypes


def mxq(x, axis, fmt="e4m3"):
    dtype, down = {"e4m3": (ml_dtypes.float8_e4m3fn, 7), "e5m2": (ml_dtypes.float8_e5m2, 14)}[fmt]
    v = np.moveaxis(np.asarray(x, np.float32).astype(ml_dtypes.bfloat16).astype(np.float64), axis, -1)
    blocks = v.reshape(v.shape[:-1] + (-1, 32))
    amax = np.abs(blocks).max(-1, keepdims=True)
    byte = np.maximum(np.where(amax > 0, np.frexp(amax)[1] - 1 + 127, 0) - down, 1)
    scale = np.exp2(byte - 127.0)
    codes = (blocks / scale).astype(np.float32).astype(dtype).astype(np.float64)
    return np.moveaxis((codes * scale).reshape(v.shape), -1, axis)


WIDE = False


def mx_kscale(k):
    if not WIDE:
        return np.ones(k)
    levels = np.array([10, -10, 5, -5, 0])
    if k % 512:
        return np.exp2(np.random.permutation(np.resize(levels, k // 32))).repeat(32)
    a = np.empty((k // 512, 16))
    for p in range(k // 512):
        a[p, :8] = np.random.permutation(np.resize(levels, 8))
        for g in range(8):
            far = levels[np.abs(levels - a[p, g]) >= 10]
            a[p, g + 8] = far[np.random.randint(len(far))]
    return np.exp2(a.ravel()).repeat(32)


BF16 = ml_dtypes.bfloat16


def bf(x):
    return np.asarray(x, np.float32).astype(BF16)


def f64(x):
    return np.asarray(x).astype(np.float64)

E4M3FN = np.array([(-1.0 if i & 128 else 1.0) * ((1.0 + (i & 7) / 8.0) * 2.0 ** (((i >> 3) & 15) - 7) if i & 120 else (i & 7) * 2.0 ** -9) for i in range(256)])


def e4m3fn_bytes(y):
    return np.clip(np.asarray(y, np.float64), -448.0, 448.0).astype(np.float32).astype(ml_dtypes.float8_e4m3fn).view(np.uint8)


def e4m3fn_values(b):
    return E4M3FN[b]


T, N, K, D = 2048, 1024, 1024, 512


def setup_inputs():
    s = mx_kscale(T)
    dy = np.random.standard_normal((T, N)) * np.random.uniform(0.5, 1.5, (T, 1)) / np.sqrt(T) / s[:, None]
    dy_scale = (np.abs(dy).max(axis=1, keepdims=True) / 448.0).astype(np.float32)
    return {"dy_bytes": e4m3fn_bytes(dy / f64(dy_scale)),
            "dy_scale": dy_scale,
            "h": bf(np.random.standard_normal((T, K)) * s[:, None]),
            "gate": bf(np.random.uniform(0.5, 1.5, (T, 1))),
            "x": bf(np.random.standard_normal((T, D)) * s[:, None]),
            "acc_w": bf(np.random.standard_normal((N, K)) * 0.5),
            "acc_v": bf(np.random.standard_normal((N, D)) * 0.5)}


def reference(dy_bytes, dy_scale, h, gate, x, acc_w, acc_v):
    dy = e4m3fn_values(dy_bytes) * np.repeat(f64(dy_scale), N, axis=1)
    dyq = mxq(dy, 0, "e4m3")
    a = f64(gate) * np.maximum(f64(h), 0.0)
    dw = dyq.T @ mxq(a, 0, "e4m3")
    dv = dyq.T @ mxq(f64(x), 0, "e4m3")
    return f64(acc_w) + dw, f64(acc_v) + dv

@@ -1,0 +1,211 @@
+from contextlib import ExitStack
+
+import concourse.mybir as mybir
+
+T, N, K, D = 2048, 1024, 1024, 512
+FLOPS = 2 * T * N * (K + D)
+
+F32 = mybir.dt.float32
+BF16 = mybir.dt.bfloat16
+U32 = mybir.dt.uint32
+U8 = mybir.dt.uint8
+FP8 = mybir.dt.float8_e4m3fn
+FP8X4 = mybir.dt.float8_e4m3fn_x4
+ALU = mybir.AluOpType
+ACT = mybir.ActivationFunctionType
+
+P = 128
+PACK = 4
+PASSES = T // (P * PACK)
+BANK = 512
+BANKS = 8
+RUN = 4
+
+CHUNKS = [["X",0,512,[0]],["D",0,512,[0]],["X",0,512,[1]],["D",0,512,[1]],["X",0,512,[2]],["D",0,512,[2]],["X",0,512,[3]],["D",0,512,[3]],["H",0,512,[0]],["H",0,512,[1]],["H",0,512,[2]],["H",0,512,[3]],["D",512,256,[0,1]],["D",512,256,[2,3]],["H",512,512,[0]],["H",512,512,[1]],["H",512,512,[2]],["H",512,512,[3]],["D",768,128,[0,1,2,3]],["D",896,128,[0,1]],["D",896,128,[2,3]]]
+INTERLEAVER = "VVVVSVSVSVSSVSSVSSVSS"
+WIDENER = "VSVSSVVSVSSVSSSVSVSSS"
+LEAD = [1,4,5,4,1,3,5,1,3,3,2,2,3,4,4,5,5,5,5,4,1]
+ILV_LEAD = [1,1,3,1,3,1,3,1,1,2,1,2,1,2,3,2,2,3,1,1,1]
+ADDS = [6,1,0,5,3,6,1,2,3,1,6,6,0,1,5,6,5,3,6,5,1]
+STAGE_BANKS = []
+LOADS = [["X",0,0,512],["D",0,0,512],["X",1,0,512],["D",1,0,1024],["X",2,0,512],["D",2,0,1024],["X",3,0,512],["D",3,0,1024],["H",0,0,1024],["H",1,0,1024],["V",0,0,4],["D",0,512,512],["H",2,0,1024],["H",3,0,1024],["W",0,0,4],["V",0,4,4],["W",0,4,4]]
+
+
+def program():
+    n = len(CHUNKS)
+    out, have, groups, nxt, finished = [], set(), [], {}, []
+    added = 0
+    seen_m, seen_n = [], []
+    for step in range(-max(LEAD + ILV_LEAD), n):
+        for j in range(n):
+            if j - LEAD[j] == step and CHUNKS[j][0] != "X":
+                out.append(("prep", j))
+        for j in range(n):
+            if j - ILV_LEAD[j] == step:
+                out.append(("ilv", j))
+        if step >= 0:
+            out.append(("quant", step))
+            for rep in range(ADDS[step]):
+                if added < len(finished):
+                    out.append(("add", finished[added]))
+                    added += 1
+            kind, c0, w, gs = CHUNKS[step]
+            for g in gs:
+                if kind == "D":
+                    for m in range(c0 // P, (c0 + w) // P):
+                        have.add((m, g))
+                else:
+                    have.add(((kind, c0), g))
+            if gs[0] == 0:
+                if kind == "D":
+                    ms = list(range(c0 // P, (c0 + w) // P))
+                    groups.extend([(m, nn) for m in ms for nn in seen_n])
+                    seen_m.extend(ms)
+                else:
+                    groups.extend([(m, (kind, c0)) for m in seen_m])
+                    seen_n.append((kind, c0))
+            for gr in groups:
+                g = nxt.get(gr, 0)
+                while g < PASSES and (gr[0], g) in have and (gr[1], g) in have:
+                    out.append(("mm", gr, g))
+                    g += 1
+                    if g == PASSES:
+                        finished.append(gr)
+                nxt[gr] = g
+    while added < len(finished):
+        out.append(("add", finished[added]))
+        added += 1
+    return out
+
+
+def tile_gated_skip_wgrad_fp8_d3_kernel(tc, dy_bytes, dy_scale, h, gate, x, acc_w, acc_v, out_0, out_1):
+    nc = tc.nc
+    prog = program()
+    last_stage = max([i for i, o in enumerate(prog) if o[0] == "ilv" and INTERLEAVER[o[1]] in "PQ"] + [-1])
+    with ExitStack() as ctx:
+        keep = ctx.enter_context(tc.tile_pool(name="keep", bufs=1))
+        planes_pool = ctx.enter_context(tc.tile_pool(name="planes", bufs=7))
+        grouped_pool = ctx.enter_context(tc.tile_pool(name="grouped", bufs=5))
+        result_pool = ctx.enter_context(tc.tile_pool(name="result", bufs=16))
+        psum = ctx.enter_context(tc.psum_pool(name="psum", bufs=1))
+        ctx.enter_context(tc.manual_schedule())
+
+        scale_sb = keep.tile([P, PASSES, PACK], F32, name="scale_sb")
+        gate_sb = keep.tile([P, PASSES, PACK], BF16, name="gate_sb")
+        nc.scalar.dma_start(out=scale_sb[:], in_=dy_scale.rearrange("(g p t) o -> p g (t o)", p=P, t=PACK))
+        nc.scalar.dma_start(out=gate_sb[:], in_=gate.rearrange("(g p t) o -> p g (t o)", p=P, t=PACK))
+
+        warm_in = keep.tile([P, 8], F32, name="warm_in")
+        warm_out = keep.tile([P, 8], F32, name="warm_out")
+        nc.vector.memset(warm_in[:], 0.0)
+        nc.scalar.activation(out=warm_out[:], in_=warm_in[:], func=ACT.Copy)
+
+        ident = None
+        raw = {}
+        accs = {}
+        for kind, idx, c0, w in LOADS:
+            if kind in "DHX":
+                src = {"D": dy_bytes, "H": h, "X": x}[kind]
+                name = {"D": "dy_codes_in", "H": "h_raw", "X": "x_raw"}[kind] + "_%d_%d" % (idx, c0)
+                tl = keep.tile([P, PACK, w], U8 if kind == "D" else BF16, name=name, align_bytes=64)
+                rows = src.rearrange("(g p t) c -> g p t c", p=P, t=PACK)[idx]
+                nc.sync.dma_start(out=tl[:], in_=rows[:, :, c0:c0 + w])
+                for c in range(c0, c0 + w, P):
+                    raw[(kind, idx, c)] = (tl, c - c0)
+            else:
+                src = acc_w if kind == "W" else acc_v
+                width = src.shape[1]
+                tl = keep.tile([P, w, width], BF16, name="acc_%s_%d" % (kind, c0), align_bytes=64)
+                nc.sync.dma_start(out=tl[:], in_=src.rearrange("(m p) c -> p m c", p=P)[:, c0:c0 + w, :])
+                for m in range(c0, c0 + w):
+                    accs[(kind, m)] = (tl, m - c0)
+
+        planes, grouped, operand = {}, {}, {}
+        bank_age = {b: -1 for b in range(BANKS)}
+        bank_of, acc_tile = {}, {}
+        staged = 0
+        for pos, op in enumerate(prog):
+            if op[0] == "prep":
+                j = op[1]
+                kind, c0, w, gs = CHUNKS[j]
+                pl = planes_pool.tile([P, PACK, w * len(gs)], BF16, name="plane", align_bytes=64)
+                planes[j] = pl[:]
+                for gi, g in enumerate(gs):
+                    tl, off = raw[(kind, g, c0)]
+                    for t in range(PACK):
+                        dst = pl[:, t, gi * w:(gi + 1) * w]
+                        src = tl[:, t, off:off + w]
+                        if kind == "H":
+                            nc.vector.tensor_scalar(out=dst, in0=src, scalar1=0.0, scalar2=gate_sb[:, g, t:t + 1], op0=ALU.max, op1=ALU.mult)
+                        elif WIDENER[j] == "S":
+                            nc.scalar.activation(out=dst, in_=src.bitcast(FP8), func=ACT.Copy, scale=scale_sb[:, g, t:t + 1])
+                        else:
+                            nc.vector.tensor_scalar(out=dst, in0=src.bitcast(FP8), scalar1=scale_sb[:, g, t:t + 1], scalar2=None, op0=ALU.mult)
+            elif op[0] == "ilv":
+                j = op[1]
+                kind, c0, w, gs = CHUNKS[j]
+                cols = w * len(gs)
+                if kind == "X":
+                    tl, off = raw[(kind, gs[0], c0)]
+                    planes[j] = tl[:, :, off:off + w]
+                gr = grouped_pool.tile([P, cols, PACK], BF16, name="group", align_bytes=64)
+                grouped[j] = gr
+                if INTERLEAVER[j] in "PQ":
+                    half = BANK // 2
+                    for c in range(0, cols, half):
+                        b = STAGE_BANKS[staged % len(STAGE_BANKS)]
+                        staged += 1
+                        st = psum.tile([P, half * PACK], BF16, name="bank%d" % b)
+                        for q in range(2):
+                            cs = slice(c + q * P, c + (q + 1) * P)
+                            nc.tensor.matmul(out=st[:, q * BANK:(q + 1) * BANK], lhsT=ident[:], rhs=planes[j][:, :, cs].rearrange("p t c -> p c t"), start=True, stop=True)
+                        dst = gr[:, c:c + half, :].rearrange("p c t -> p (c t)")
+                        if INTERLEAVER[j] == "P":
+                            nc.scalar.copy(out=dst, in_=st[:])
+                        else:
+                            nc.vector.tensor_copy(out=dst, in_=st[:])
+                        bank_age[b] = pos
+                else:
+                    dst = gr[:].rearrange("p (c i) t -> p c t i", i=RUN)
+                    src = planes[j].rearrange("p t (c i) -> p c t i", i=RUN)
+                    if INTERLEAVER[j] == "V":
+                        nc.vector.tensor_copy(out=dst, in_=src)
+                    elif INTERLEAVER[j] == "S":
+                        nc.scalar.copy(out=dst, in_=src)
+                    else:
+                        nc.gpsimd.tensor_scalar(out=dst, in0=src, scalar1=1.0, scalar2=0.0, op0=ALU.mult, op1=ALU.add)
+            elif op[0] == "quant":
+                j = op[1]
+                kind, c0, w, gs = CHUNKS[j]
+                cols = w * len(gs)
+                codes = keep.tile([P, cols], U32, name="codes%d" % j, align_bytes=64)
+                scales = keep.tile([P, cols], U8, name="scales%d" % j, align_bytes=64)
+                nc.vector.quantize_mx(out=codes[:].bitcast(FP8X4), scales=scales[:], in_=grouped[j][:].rearrange("p c t -> p (c t)"))
+                for gi, g in enumerate(gs):
+                    if kind == "D":
+                        for m in range(w // P):
+                            cs = slice(gi * w + m * P, gi * w + (m + 1) * P)
+                            operand[(c0 // P + m, g)] = (codes[:, cs], scales[:, cs])
+                    else:
+                        cs = slice(gi * w, (gi + 1) * w)
+                        operand[((kind, c0), g)] = (codes[:, cs], scales[:, cs])
+            elif op[0] == "mm":
+                grp, g = op[1], op[2]
+                if g == 0:
+                    free = [b for b in range(BANKS) if (pos > last_stage or b not in STAGE_BANKS) and b not in bank_of.values()]
+                    b = min(free, key=lambda bb: bank_age[bb])
+                    bank_of[grp] = b
+                    acc_tile[grp] = psum.tile([P, BANK], F32, name="bank%d" % b)
+                lhs, lhs_scale = operand[(grp[0], g)]
+                rhs, rhs_scale = operand[(grp[1], g)]
+                nc.tensor.matmul_mx(out=acc_tile[grp][:], lhsT=lhs.bitcast(FP8X4), lhsT_scale=lhs_scale, rhs=rhs.bitcast(FP8X4), rhs_scale=rhs_scale,
+                                    start=(g == 0), stop=(g == PASSES - 1))
+            else:
+                grp = op[1]
+                m, (kind, c0) = grp
+                tl, mi = accs[("V" if kind == "X" else "W", m)]
+                res = result_pool.tile([P, BANK], F32, name="res")
+                nc.vector.tensor_tensor(out=res[:], in0=acc_tile[grp][:], in1=tl[:, mi, c0:c0 + BANK], op=ALU.add)
+                dst = out_1 if kind == "X" else out_0
+                nc.sync.dma_start(out=dst[m * P:(m + 1) * P, c0:c0 + BANK], in_=res[:])
+                bank_age[bank_of.pop(grp)] = pos

@@ -1,6 +1,7 @@
 from contextlib import ExitStack
 
 import concourse.mybir as mybir
+from concourse.masks import make_identity
 
 T, N, K, D = 2048, 1024, 1024, 512
 FLOPS = 2 * T * N * (K + D)
@@ -22,13 +23,13 @@ BANKS = 8
 RUN = 4
 
 CHUNKS = [["X",0,512,[0]],["D",0,512,[0]],["X",0,512,[1]],["D",0,512,[1]],["X",0,512,[2]],["D",0,512,[2]],["X",0,512,[3]],["D",0,512,[3]],["H",0,512,[0]],["H",0,512,[1]],["H",0,512,[2]],["H",0,512,[3]],["D",512,256,[0,1]],["D",512,256,[2,3]],["H",512,512,[0]],["H",512,512,[1]],["H",512,512,[2]],["H",512,512,[3]],["D",768,128,[0,1,2,3]],["D",896,128,[0,1]],["D",896,128,[2,3]]]
-INTERLEAVER = "VVVVSVSVSVSSVSSVSSVSS"
-WIDENER = "VSVSSVVSVSSVSSSVSVSSS"
-LEAD = [1,4,5,4,1,3,5,1,3,3,2,2,3,4,4,5,5,5,5,4,1]
-ILV_LEAD = [1,1,3,1,3,1,3,1,1,2,1,2,1,2,3,2,2,3,1,1,1]
-ADDS = [6,1,0,5,3,6,1,2,3,1,6,6,0,1,5,6,5,3,6,5,1]
-STAGE_BANKS = []
-LOADS = [["X",0,0,512],["D",0,0,512],["X",1,0,512],["D",1,0,1024],["X",2,0,512],["D",2,0,1024],["X",3,0,512],["D",3,0,1024],["H",0,0,1024],["H",1,0,1024],["V",0,0,4],["D",0,512,512],["H",2,0,1024],["H",3,0,1024],["W",0,0,4],["V",0,4,4],["W",0,4,4]]
+INTERLEAVER = "SVSPPVSPPPPPPSSPSVSSS"
+WIDENER = "SVVSSVSVVVVSVSVVVVSSS"
+LEAD = [4,2,4,3,5,4,2,5,4,3,2,2,4,5,3,3,4,3,1,1,2]
+ILV_LEAD = [3,2,2,3,3,2,2,3,3,1,2,1,3,2,3,2,3,1,1,1,1]
+ADDS = [2,5,2,1,0,3,5,6,3,4,6,4,3,5,5,2,3,0,5,5,6]
+MM_DELAY = [1,0,1,1,0,1,2,1,2,1,1,1,2,1,1,1,0,0,2,2,2]
+LOADS = [["X",0,0,512],["D",0,0,512],["D",1,0,1024],["X",1,0,512],["D",2,0,1024],["X",2,0,512],["D",3,0,1024],["X",3,0,512],["H",0,0,1024],["H",1,0,1024],["H",2,0,1024],["D",0,512,512],["H",3,0,1024],["V",0,0,512],["W",0,0,1024],["V",1,0,512],["W",1,0,1024]]
 
 
 def program():
@@ -49,7 +50,8 @@ def program():
                 if added < len(finished):
                     out.append(("add", finished[added]))
                     added += 1
-            kind, c0, w, gs = CHUNKS[step]
+        for j in [jj for jj in range(n) if jj + MM_DELAY[jj] == step or (step == n - 1 and jj + MM_DELAY[jj] > step)]:
+            kind, c0, w, gs = CHUNKS[j]
             for g in gs:
                 if kind == "D":
                     for m in range(c0 // P, (c0 + w) // P):
@@ -81,7 +83,6 @@ def program():
 def tile_gated_skip_wgrad_fp8_d3_kernel(tc, dy_bytes, dy_scale, h, gate, x, acc_w, acc_v, out_0, out_1):
     nc = tc.nc
     prog = program()
-    last_stage = max([i for i, o in enumerate(prog) if o[0] == "ilv" and INTERLEAVER[o[1]] in "PQ"] + [-1])
     with ExitStack() as ctx:
         keep = ctx.enter_context(tc.tile_pool(name="keep", bufs=1))
         planes_pool = ctx.enter_context(tc.tile_pool(name="planes", bufs=7))
@@ -99,8 +100,9 @@ def tile_gated_skip_wgrad_fp8_d3_kernel(tc, dy_bytes, dy_scale, h, gate, x, acc_
         warm_out = keep.tile([P, 8], F32, name="warm_out")
         nc.vector.memset(warm_in[:], 0.0)
         nc.scalar.activation(out=warm_out[:], in_=warm_in[:], func=ACT.Copy)
+        ident = keep.tile([P, P], BF16, name="ident")
+        make_identity(nc, ident[:])
 
-        ident = None
         raw = {}
         accs = {}
         for kind, idx, c0, w in LOADS:
@@ -114,16 +116,16 @@ def tile_gated_skip_wgrad_fp8_d3_kernel(tc, dy_bytes, dy_scale, h, gate, x, acc_
                     raw[(kind, idx, c)] = (tl, c - c0)
             else:
                 src = acc_w if kind == "W" else acc_v
-                width = src.shape[1]
-                tl = keep.tile([P, w, width], BF16, name="acc_%s_%d" % (kind, c0), align_bytes=64)
-                nc.sync.dma_start(out=tl[:], in_=src.rearrange("(m p) c -> p m c", p=P)[:, c0:c0 + w, :])
-                for m in range(c0, c0 + w):
-                    accs[(kind, m)] = (tl, m - c0)
+                tl = keep.tile([P, 4, w], BF16, name="acc_%s_%d_%d" % (kind, idx, c0), align_bytes=64)
+                nc.sync.dma_start(out=tl[:], in_=src.rearrange("(m p) c -> p m c", p=P)[:, 4 * idx:4 * idx + 4, c0:c0 + w])
+                for m in range(4):
+                    for c in range(c0, c0 + w, BANK):
+                        accs[(kind, 4 * idx + m, c)] = tl[:, m, c - c0:c - c0 + BANK]
 
         planes, grouped, operand = {}, {}, {}
         bank_age = {b: -1 for b in range(BANKS)}
         bank_of, acc_tile = {}, {}
-        staged = 0
+        tick = 0
         for pos, op in enumerate(prog):
             if op[0] == "prep":
                 j = op[1]
@@ -153,8 +155,7 @@ def tile_gated_skip_wgrad_fp8_d3_kernel(tc, dy_bytes, dy_scale, h, gate, x, acc_
                 if INTERLEAVER[j] in "PQ":
                     half = BANK // 2
                     for c in range(0, cols, half):
-                        b = STAGE_BANKS[staged % len(STAGE_BANKS)]
-                        staged += 1
+                        b = min([bb for bb in range(BANKS) if bb not in bank_of.values()], key=lambda bb: bank_age[bb])
                         st = psum.tile([P, half * PACK], BF16, name="bank%d" % b)
                         for q in range(2):
                             cs = slice(c + q * P, c + (q + 1) * P)
@@ -164,7 +165,8 @@ def tile_gated_skip_wgrad_fp8_d3_kernel(tc, dy_bytes, dy_scale, h, gate, x, acc_
                             nc.scalar.copy(out=dst, in_=st[:])
                         else:
                             nc.vector.tensor_copy(out=dst, in_=st[:])
-                        bank_age[b] = pos
+                        tick += 1
+                        bank_age[b] = tick
                 else:
                     dst = gr[:].rearrange("p (c i) t -> p c t i", i=RUN)
                     src = planes[j].rearrange("p t (c i) -> p c t i", i=RUN)
@@ -192,7 +194,7 @@ def tile_gated_skip_wgrad_fp8_d3_kernel(tc, dy_bytes, dy_scale, h, gate, x, acc_
             elif op[0] == "mm":
                 grp, g = op[1], op[2]
                 if g == 0:
-                    free = [b for b in range(BANKS) if (pos > last_stage or b not in STAGE_BANKS) and b not in bank_of.values()]
+                    free = [b for b in range(BANKS) if b not in bank_of.values()]
                     b = min(free, key=lambda bb: bank_age[bb])
                     bank_of[grp] = b
                     acc_tile[grp] = psum.tile([P, BANK], F32, name="bank%d" % b)
@@ -203,9 +205,9 @@ def tile_gated_skip_wgrad_fp8_d3_kernel(tc, dy_bytes, dy_scale, h, gate, x, acc_
             else:
                 grp = op[1]
                 m, (kind, c0) = grp
-                tl, mi = accs[("V" if kind == "X" else "W", m)]
                 res = result_pool.tile([P, BANK], F32, name="res")
-                nc.vector.tensor_tensor(out=res[:], in0=acc_tile[grp][:], in1=tl[:, mi, c0:c0 + BANK], op=ALU.add)
+                nc.vector.tensor_tensor(out=res[:], in0=acc_tile[grp][:], in1=accs[("V" if kind == "X" else "W", m, c0)], op=ALU.add)
                 dst = out_1 if kind == "X" else out_0
                 nc.sync.dma_start(out=dst[m * P:(m + 1) * P, c0:c0 + BANK], in_=res[:])
-                bank_age[bank_of.pop(grp)] = pos
+                tick += 1
+                bank_age[bank_of.pop(grp)] = tick

@@ -21,62 +21,52 @@ PASSES = T // (P * PACK)
 BANK = 512
 BANKS = 8
 RUN = 4
+PE_RUN = 8
 
 CHUNKS = [["X",0,512,[0]],["D",0,512,[0]],["X",0,512,[1]],["D",0,512,[1]],["X",0,512,[2]],["D",0,512,[2]],["X",0,512,[3]],["D",0,512,[3]],["H",0,512,[0]],["H",0,512,[1]],["H",0,512,[2]],["H",0,512,[3]],["D",512,256,[0,1]],["D",512,256,[2,3]],["H",512,512,[0]],["H",512,512,[1]],["H",512,512,[2]],["H",512,512,[3]],["D",768,128,[0,1,2,3]],["D",896,128,[0,1]],["D",896,128,[2,3]]]
-INTERLEAVER = "SVSPPVSPPPPPPSSPSVSSS"
-WIDENER = "SVVSSVSVVVVSVSVVVVSSS"
-LEAD = [4,2,4,3,5,4,2,5,4,3,2,2,4,5,3,3,4,3,1,1,2]
-ILV_LEAD = [3,2,2,3,3,2,2,3,3,1,2,1,3,2,3,2,3,1,1,1,1]
-ADDS = [2,5,2,1,0,3,5,6,3,4,6,4,3,5,5,2,3,0,5,5,6]
-MM_DELAY = [1,0,1,1,0,1,2,1,2,1,1,1,2,1,1,1,0,0,2,2,2]
-LOADS = [["X",0,0,512],["D",0,0,512],["D",1,0,1024],["X",1,0,512],["D",2,0,1024],["X",2,0,512],["D",3,0,1024],["X",3,0,512],["H",0,0,1024],["H",1,0,1024],["H",2,0,1024],["D",0,512,512],["H",3,0,1024],["V",0,0,512],["W",0,0,1024],["V",1,0,512],["W",1,0,1024]]
+INTERLEAVER = "PVVPPVPPPSVSVSSSSVSSS"
+WIDENER = "VVVSSVVSSSSVVSVVSVSSS"
+ORDER = "p1 p3 p7 i1 p12 p5 i12 p13 i5 q12 q1 i3 q3 i7 q5 q7 p8 i2 i13 i0 q13 q2 p15 p9 i4 i6 q0 i9 i8 m0 q4 m1 m2 p14 p11 q6 m3 m4 i11 p10 q8 i10 q9 i15 m5 q10 m6 m7 q11 m8 m9 m10 a m11 p16 i14 a a a m12 m13 a i16 a q15 a p18 q14 a a i18 a m14 p17 p19 q16 p20 i17 m15 q17 i19 a q18 m16 m17 a a a m18 i20 a a a q19 a a m19 q20 a a m20 a a a"
+VIA_GPSIMD = [0,0,0,0,0,0,0,0,0,0,0,0,0,0,0,0,0,0,0,0,0,0,0,0]
+LOADS = [["D",0,0,512],["D",1,0,1024],["D",0,512,512],["D",3,0,1024],["D",2,0,1024],["X",0,0,512],["H",0,0,1024],["X",3,0,512],["X",2,0,512],["X",1,0,512],["H",1,0,1024],["H",3,0,1024],["H",2,0,1024],["W",0,0,1024],["V",0,0,512],["W",1,0,1024],["V",1,0,512]]
 
 
 def program():
-    n = len(CHUNKS)
     out, have, groups, nxt, finished = [], set(), [], {}, []
     added = 0
     seen_m, seen_n = [], []
-    for step in range(-max(LEAD + ILV_LEAD), n):
-        for j in range(n):
-            if j - LEAD[j] == step and CHUNKS[j][0] != "X":
-                out.append(("prep", j))
-        for j in range(n):
-            if j - ILV_LEAD[j] == step:
-                out.append(("ilv", j))
-        if step >= 0:
-            out.append(("quant", step))
-            for rep in range(ADDS[step]):
-                if added < len(finished):
-                    out.append(("add", finished[added]))
-                    added += 1
-        for j in [jj for jj in range(n) if jj + MM_DELAY[jj] == step or (step == n - 1 and jj + MM_DELAY[jj] > step)]:
-            kind, c0, w, gs = CHUNKS[j]
-            for g in gs:
-                if kind == "D":
-                    for m in range(c0 // P, (c0 + w) // P):
-                        have.add((m, g))
-                else:
-                    have.add(((kind, c0), g))
-            if gs[0] == 0:
-                if kind == "D":
-                    ms = list(range(c0 // P, (c0 + w) // P))
-                    groups.extend([(m, nn) for m in ms for nn in seen_n])
-                    seen_m.extend(ms)
-                else:
-                    groups.extend([(m, (kind, c0)) for m in seen_m])
-                    seen_n.append((kind, c0))
-            for gr in groups:
-                g = nxt.get(gr, 0)
-                while g < PASSES and (gr[0], g) in have and (gr[1], g) in have:
-                    out.append(("mm", gr, g))
-                    g += 1
-                    if g == PASSES:
-                        finished.append(gr)
-                nxt[gr] = g
-    while added < len(finished):
-        out.append(("add", finished[added]))
-        added += 1
+    for token in ORDER.split():
+        if token == "a":
+            out.append(("add", finished[added]))
+            added += 1
+            continue
+        j = int(token[1:])
+        if token[0] != "m":
+            out.append(({"p": "prep", "i": "ilv", "q": "quant"}[token[0]], j))
+            continue
+        kind, c0, w, gs = CHUNKS[j]
+        for g in gs:
+            if kind == "D":
+                for m in range(c0 // P, (c0 + w) // P):
+                    have.add((m, g))
+            else:
+                have.add(((kind, c0), g))
+        if gs[0] == 0:
+            if kind == "D":
+                ms = list(range(c0 // P, (c0 + w) // P))
+                groups.extend([(m, nn) for m in ms for nn in seen_n])
+                seen_m.extend(ms)
+            else:
+                groups.extend([(m, (kind, c0)) for m in seen_m])
+                seen_n.append((kind, c0))
+        for gr in groups:
+            g = nxt.get(gr, 0)
+            while g < PASSES and (gr[0], g) in have and (gr[1], g) in have:
+                out.append(("mm", gr, g))
+                g += 1
+                if g == PASSES:
+                    finished.append(gr)
+            nxt[gr] = g
     return out
 
 
@@ -126,6 +116,7 @@ def tile_gated_skip_wgrad_fp8_d3_kernel(tc, dy_bytes, dy_scale, h, gate, x, acc_
         bank_age = {b: -1 for b in range(BANKS)}
         bank_of, acc_tile = {}, {}
         tick = 0
+        n_added = 0
         for pos, op in enumerate(prog):
             if op[0] == "prep":
                 j = op[1]
@@ -159,7 +150,8 @@ def tile_gated_skip_wgrad_fp8_d3_kernel(tc, dy_bytes, dy_scale, h, gate, x, acc_
                         st = psum.tile([P, half * PACK], BF16, name="bank%d" % b)
                         for q in range(2):
                             cs = slice(c + q * P, c + (q + 1) * P)
-                            nc.tensor.matmul(out=st[:, q * BANK:(q + 1) * BANK], lhsT=ident[:], rhs=planes[j][:, :, cs].rearrange("p t c -> p c t"), start=True, stop=True)
+                            nc.tensor.matmul(out=st[:, q * BANK:(q + 1) * BANK].rearrange("p (c i t) -> p c t i", i=PE_RUN, t=PACK), lhsT=ident[:],
+                                             rhs=planes[j][:, :, cs].rearrange("p t (c i) -> p c t i", i=PE_RUN), start=True, stop=True)
                         dst = gr[:, c:c + half, :].rearrange("p c t -> p (c t)")
                         if INTERLEAVER[j] == "P":
                             nc.scalar.copy(out=dst, in_=st[:])
@@ -170,12 +162,16 @@ def tile_gated_skip_wgrad_fp8_d3_kernel(tc, dy_bytes, dy_scale, h, gate, x, acc_
                 else:
                     dst = gr[:].rearrange("p (c i) t -> p c t i", i=RUN)
                     src = planes[j].rearrange("p t (c i) -> p c t i", i=RUN)
-                    if INTERLEAVER[j] == "V":
-                        nc.vector.tensor_copy(out=dst, in_=src)
-                    elif INTERLEAVER[j] == "S":
-                        nc.scalar.copy(out=dst, in_=src)
-                    else:
-                        nc.gpsimd.tensor_scalar(out=dst, in0=src, scalar1=1.0, scalar2=0.0, op0=ALU.mult, op1=ALU.add)
+                    runs = cols // RUN
+                    cut = {"V": 0, "S": 0, "G": runs, "g": 3 * runs // 4, "h": 3 * runs // 4}[INTERLEAVER[j]]
+                    if cut > 0:
+                        nc.gpsimd.tensor_scalar(out=gr[:, 0:cut * RUN, :], in0=planes[j][:, :, 0:cut * RUN].rearrange("p t c -> p c t"),
+                                                scalar1=1.0, scalar2=0.0, op0=ALU.mult, op1=ALU.add)
+                    if cut < runs:
+                        if INTERLEAVER[j] in "Vh":
+                            nc.vector.tensor_copy(out=dst[:, cut:runs], in_=src[:, cut:runs])
+                        else:
+                            nc.scalar.copy(out=dst[:, cut:runs], in_=src[:, cut:runs])
             elif op[0] == "quant":
                 j = op[1]
                 kind, c0, w, gs = CHUNKS[j]
@@ -206,8 +202,19 @@ def tile_gated_skip_wgrad_fp8_d3_kernel(tc, dy_bytes, dy_scale, h, gate, x, acc_
                 grp = op[1]
                 m, (kind, c0) = grp
                 res = result_pool.tile([P, BANK], F32, name="res")
-                nc.vector.tensor_tensor(out=res[:], in0=acc_tile[grp][:], in1=accs[("V" if kind == "X" else "W", m, c0)], op=ALU.add)
-                dst = out_1 if kind == "X" else out_0
-                nc.sync.dma_start(out=dst[m * P:(m + 1) * P, c0:c0 + BANK], in_=res[:])
+                dst = (out_1 if kind == "X" else out_0)[m * P:(m + 1) * P, c0:c0 + BANK]
+                prior = accs[("V" if kind == "X" else "W", m, c0)]
+                if VIA_GPSIMD[n_added]:
+                    sums = grouped_pool.tile([P, BANK], F32, name="sums", bufs=2)
+                    nc.scalar.copy(out=sums[:], in_=acc_tile[grp][:])
+                    nc.gpsimd.tensor_tensor(out=res[:], in0=sums[:], in1=prior, op=ALU.add)
+                    nc.sync.dma_start(out=dst, in_=res[:])
+                else:
+                    pieces = 2 if n_added == len(VIA_GPSIMD) - 1 else 1
+                    for q in range(pieces):
+                        cs = slice(q * BANK // pieces, (q + 1) * BANK // pieces)
+                        nc.vector.tensor_tensor(out=res[:, cs], in0=acc_tile[grp][:, cs], in1=prior[:, cs], op=ALU.add)
+                        nc.sync.dma_start(out=dst[:, cs], in_=res[:, cs])
+                n_added += 1
                 tick += 1
                 bank_age[bank_of.pop(grp)] = tick

@@ -20,64 +20,93 @@ PACK = 4
 PASSES = T // (P * PACK)
 BANK = 512
 BANKS = 8
-RUN = 4
-PE_RUN = 8
+GROUPS = (N // P) * ((K + D) // BANK)
+ACC_ROWS = 4
+COPY_RUN = 4
+MATMUL_RUN = 8
+PLANE_BUFS = 7
+WOVEN_BUFS = 5
 
-CHUNKS = [["X",0,512,[0]],["D",0,512,[0]],["X",0,512,[1]],["D",0,512,[1]],["X",0,512,[2]],["D",0,512,[2]],["X",0,512,[3]],["D",0,512,[3]],["H",0,512,[0]],["H",0,512,[1]],["H",0,512,[2]],["H",0,512,[3]],["D",512,256,[0,1]],["D",512,256,[2,3]],["H",512,512,[0]],["H",512,512,[1]],["H",512,512,[2]],["H",512,512,[3]],["D",768,128,[0,1,2,3]],["D",896,128,[0,1]],["D",896,128,[2,3]]]
-INTERLEAVER = "PVVPPVPPPSVSVSSSSVSSS"
-WIDENER = "VVVSSVVSSSSVVSVVSVSSS"
-ORDER = "p1 p3 p7 i1 p12 p5 i12 p13 i5 q12 q1 i3 q3 i7 q5 q7 p8 i2 i13 i0 q13 q2 p15 p9 i4 i6 q0 i9 i8 m0 q4 m1 m2 p14 p11 q6 m3 m4 i11 p10 q8 i10 q9 i15 m5 q10 m6 m7 q11 m8 m9 m10 a m11 p16 i14 a a a m12 m13 a i16 a q15 a p18 q14 a a i18 a m14 p17 p19 q16 p20 i17 m15 q17 i19 a q18 m16 m17 a a a m18 i20 a a a q19 a a m19 q20 a a m20 a a a"
-VIA_GPSIMD = [0,0,0,0,0,0,0,0,0,0,0,0,0,0,0,0,0,0,0,0,0,0,0,0]
-LOADS = [["D",0,0,512],["D",1,0,1024],["D",0,512,512],["D",3,0,1024],["D",2,0,1024],["X",0,0,512],["H",0,0,1024],["X",3,0,512],["X",2,0,512],["X",1,0,512],["H",1,0,1024],["H",3,0,1024],["H",2,0,1024],["W",0,0,1024],["V",0,0,512],["W",1,0,1024],["V",1,0,512]]
+CHUNKS = {
+    "x0": ("x", 0, 512, [0]), "dyA0": ("dy", 0, 512, [0]),
+    "x1": ("x", 0, 512, [1]), "dyA1": ("dy", 0, 512, [1]),
+    "x2": ("x", 0, 512, [2]), "dyA2": ("dy", 0, 512, [2]),
+    "x3": ("x", 0, 512, [3]), "dyA3": ("dy", 0, 512, [3]),
+    "aA0": ("h", 0, 512, [0]), "aA1": ("h", 0, 512, [1]), "aA2": ("h", 0, 512, [2]), "aA3": ("h", 0, 512, [3]),
+    "dyB0": ("dy", 512, 256, [0, 1]), "dyB1": ("dy", 512, 256, [2, 3]),
+    "aB0": ("h", 512, 512, [0]), "aB1": ("h", 512, 512, [1]), "aB2": ("h", 512, 512, [2]), "aB3": ("h", 512, 512, [3]),
+    "dyC": ("dy", 768, 128, [0, 1, 2, 3]),
+    "dyD0": ("dy", 896, 128, [0, 1]), "dyD1": ("dy", 896, 128, [2, 3]),
+}
+
+WOVEN_BY_VECTOR = ["x0", "dyA0", "x1", "dyA2", "aA1", "aA2", "aB3"]
+WOVEN_BY_TENSOR = ["dyA1", "x2", "dyA3", "aA0", "dyB0"]
+WIDENED_BY_VECTOR = ["dyA0", "dyA1"]
+
+LOADS = [
+    ("dy", 0, 0, 512), ("dy", 3, 0, 1024), ("dy", 1, 0, 1024), ("dy", 2, 0, 1024),
+    ("x", 1, 0, 512), ("x", 0, 0, 512), ("x", 3, 0, 512), ("x", 2, 0, 512),
+    ("dy", 0, 512, 512), ("h", 0, 0, 1024), ("h", 3, 0, 1024), ("h", 1, 0, 1024),
+    ("h", 2, 0, 1024), ("acc_v", 0, 0, 512), ("acc_w", 0, 0, 1024), ("acc_v", 1, 0, 512),
+    ("acc_w", 1, 0, 1024),
+]
+
+ORDER = """
+prep:dyA3 prep:dyA0 prep:dyA1 weave:dyA0 prep:dyA2 prep:dyB1 weave:x1 weave:x0 weave:dyA2 quant:dyA0
+quant:dyA2 quant:x0 weave:dyA3 weave:dyA1 quant:dyA1 weave:x3 weave:x2 prep:dyB0 mm:x0 quant:dyA3
+mm:dyA0 quant:x1 prep:aA0 quant:x3 mm:x1 prep:aA3 quant:x2 mm:dyA1 prep:aA1 prep:aA2 weave:aA0 mm:x2
+weave:aA1 weave:aA3 weave:dyB0 mm:dyA2 quant:aA0 mm:x3 mm:dyA3 weave:aA2 quant:aA1 weave:dyB1
+quant:aA2 mm:aA0 mm:aA1 add quant:aA3 add quant:dyB0 weave:aB0 weave:aB2 quant:dyB1 add mm:aA2 add
+mm:aA3 add mm:dyB0 weave:aB1 mm:dyB1 prep:dyC quant:aB0 add add add add add mm:aB0 quant:aB1 mm:aB1
+quant:aB2 weave:aB3 quant:aB3 weave:dyC add prep:dyD0 mm:aB2 add quant:dyC mm:aB3 prep:dyD1 add add
+weave:dyD0 weave:dyD1 add add add mm:dyC quant:dyD0 add add quant:dyD1 mm:dyD0 mm:dyD1 add add add
+add add
+"""
 
 
 def program():
-    out, have, groups, nxt, finished = [], set(), [], {}, []
+    steps, ready, tiles, next_pass, finished = [], set(), [], {}, []
+    row_tiles, moving = [], []
     added = 0
-    seen_m, seen_n = [], []
     for token in ORDER.split():
-        if token == "a":
-            out.append(("add", finished[added]))
+        if token == "add":
+            steps.append(("add", finished[added], added == GROUPS - 1))
             added += 1
             continue
-        j = int(token[1:])
-        if token[0] != "m":
-            out.append(({"p": "prep", "i": "ilv", "q": "quant"}[token[0]], j))
+        step, chunk = token.split(":")
+        if step != "mm":
+            steps.append((step, chunk))
             continue
-        kind, c0, w, gs = CHUNKS[j]
-        for g in gs:
-            if kind == "D":
-                for m in range(c0 // P, (c0 + w) // P):
-                    have.add((m, g))
+        operand, c0, width, passes = CHUNKS[chunk]
+        keys = list(range(c0 // P, (c0 + width) // P)) if operand == "dy" else [(operand, c0)]
+        for key in keys:
+            for g in passes:
+                ready.add((key, g))
+        if passes[0] == 0:
+            if operand == "dy":
+                tiles.extend([(m, n) for m in keys for n in moving])
+                row_tiles.extend(keys)
             else:
-                have.add(((kind, c0), g))
-        if gs[0] == 0:
-            if kind == "D":
-                ms = list(range(c0 // P, (c0 + w) // P))
-                groups.extend([(m, nn) for m in ms for nn in seen_n])
-                seen_m.extend(ms)
-            else:
-                groups.extend([(m, (kind, c0)) for m in seen_m])
-                seen_n.append((kind, c0))
-        for gr in groups:
-            g = nxt.get(gr, 0)
-            while g < PASSES and (gr[0], g) in have and (gr[1], g) in have:
-                out.append(("mm", gr, g))
+                tiles.extend([(m, keys[0]) for m in row_tiles])
+                moving.extend(keys)
+        for tile in tiles:
+            g = next_pass.get(tile, 0)
+            while g < PASSES and (tile[0], g) in ready and (tile[1], g) in ready:
+                steps.append(("pass", tile, g))
                 g += 1
                 if g == PASSES:
-                    finished.append(gr)
-            nxt[gr] = g
-    return out
+                    finished.append(tile)
+            next_pass[tile] = g
+    return steps
 
 
 def tile_gated_skip_wgrad_fp8_d3_kernel(tc, dy_bytes, dy_scale, h, gate, x, acc_w, acc_v, out_0, out_1):
     nc = tc.nc
-    prog = program()
     with ExitStack() as ctx:
         keep = ctx.enter_context(tc.tile_pool(name="keep", bufs=1))
-        planes_pool = ctx.enter_context(tc.tile_pool(name="planes", bufs=7))
-        grouped_pool = ctx.enter_context(tc.tile_pool(name="grouped", bufs=5))
-        result_pool = ctx.enter_context(tc.tile_pool(name="result", bufs=16))
+        plane_pool = ctx.enter_context(tc.tile_pool(name="planes", bufs=PLANE_BUFS))
+        woven_pool = ctx.enter_context(tc.tile_pool(name="woven", bufs=WOVEN_BUFS))
+        result_pool = ctx.enter_context(tc.tile_pool(name="result", bufs=GROUPS))
         psum = ctx.enter_context(tc.psum_pool(name="psum", bufs=1))
         ctx.enter_context(tc.manual_schedule())
 
@@ -86,135 +115,114 @@ def tile_gated_skip_wgrad_fp8_d3_kernel(tc, dy_bytes, dy_scale, h, gate, x, acc_
         nc.scalar.dma_start(out=scale_sb[:], in_=dy_scale.rearrange("(g p t) o -> p g (t o)", p=P, t=PACK))
         nc.scalar.dma_start(out=gate_sb[:], in_=gate.rearrange("(g p t) o -> p g (t o)", p=P, t=PACK))
 
-        warm_in = keep.tile([P, 8], F32, name="warm_in")
-        warm_out = keep.tile([P, 8], F32, name="warm_out")
-        nc.vector.memset(warm_in[:], 0.0)
-        nc.scalar.activation(out=warm_out[:], in_=warm_in[:], func=ACT.Copy)
+        ident_f32 = keep.tile([P, P], F32, name="ident_f32")
         ident = keep.tile([P, P], BF16, name="ident")
-        make_identity(nc, ident[:])
+        make_identity(nc, ident_f32[:])
+        nc.scalar.activation(out=ident[:], in_=ident_f32[:], func=ACT.Copy)
 
-        raw = {}
-        accs = {}
-        for kind, idx, c0, w in LOADS:
-            if kind in "DHX":
-                src = {"D": dy_bytes, "H": h, "X": x}[kind]
-                name = {"D": "dy_codes_in", "H": "h_raw", "X": "x_raw"}[kind] + "_%d_%d" % (idx, c0)
-                tl = keep.tile([P, PACK, w], U8 if kind == "D" else BF16, name=name, align_bytes=64)
-                rows = src.rearrange("(g p t) c -> g p t c", p=P, t=PACK)[idx]
-                nc.sync.dma_start(out=tl[:], in_=rows[:, :, c0:c0 + w])
-                for c in range(c0, c0 + w, P):
-                    raw[(kind, idx, c)] = (tl, c - c0)
+        loaded, prior = {}, {}
+        for tensor, index, c0, width in LOADS:
+            label = "%s_in_%d_%d" % (tensor, index, c0)
+            if tensor in ("acc_w", "acc_v"):
+                rows = (acc_w if tensor == "acc_w" else acc_v).rearrange("(m p) c -> p m c", p=P)
+                m0 = index * ACC_ROWS
+                dst = keep.tile([P, ACC_ROWS, width], BF16, name=label, align_bytes=64)
+                nc.sync.dma_start(out=dst[:], in_=rows[:, m0:m0 + ACC_ROWS, c0:c0 + width])
+                for m in range(ACC_ROWS):
+                    for c in range(0, width, BANK):
+                        prior[(tensor, m0 + m, c0 + c)] = dst[:, m, c:c + BANK]
             else:
-                src = acc_w if kind == "W" else acc_v
-                tl = keep.tile([P, 4, w], BF16, name="acc_%s_%d_%d" % (kind, idx, c0), align_bytes=64)
-                nc.sync.dma_start(out=tl[:], in_=src.rearrange("(m p) c -> p m c", p=P)[:, 4 * idx:4 * idx + 4, c0:c0 + w])
-                for m in range(4):
-                    for c in range(c0, c0 + w, BANK):
-                        accs[(kind, 4 * idx + m, c)] = tl[:, m, c - c0:c - c0 + BANK]
+                rows = {"dy": dy_bytes, "h": h, "x": x}[tensor].rearrange("(g p t) c -> g p t c", p=P, t=PACK)
+                dst = keep.tile([P, PACK, width], U8 if tensor == "dy" else BF16, name=label, align_bytes=64)
+                nc.sync.dma_start(out=dst[:], in_=rows[index][:, :, c0:c0 + width])
+                for c in range(0, width, P):
+                    loaded[(tensor, index, c0 + c)] = dst[:, :, c:width]
 
-        planes, grouped, operand = {}, {}, {}
-        bank_age = {b: -1 for b in range(BANKS)}
-        bank_of, acc_tile = {}, {}
-        tick = 0
-        n_added = 0
-        for pos, op in enumerate(prog):
-            if op[0] == "prep":
-                j = op[1]
-                kind, c0, w, gs = CHUNKS[j]
-                pl = planes_pool.tile([P, PACK, w * len(gs)], BF16, name="plane", align_bytes=64)
-                planes[j] = pl[:]
-                for gi, g in enumerate(gs):
-                    tl, off = raw[(kind, g, c0)]
-                    for t in range(PACK):
-                        dst = pl[:, t, gi * w:(gi + 1) * w]
-                        src = tl[:, t, off:off + w]
-                        if kind == "H":
-                            nc.vector.tensor_scalar(out=dst, in0=src, scalar1=0.0, scalar2=gate_sb[:, g, t:t + 1], op0=ALU.max, op1=ALU.mult)
-                        elif WIDENER[j] == "S":
-                            nc.scalar.activation(out=dst, in_=src.bitcast(FP8), func=ACT.Copy, scale=scale_sb[:, g, t:t + 1])
-                        else:
-                            nc.vector.tensor_scalar(out=dst, in0=src.bitcast(FP8), scalar1=scale_sb[:, g, t:t + 1], scalar2=None, op0=ALU.mult)
-            elif op[0] == "ilv":
-                j = op[1]
-                kind, c0, w, gs = CHUNKS[j]
-                cols = w * len(gs)
-                if kind == "X":
-                    tl, off = raw[(kind, gs[0], c0)]
-                    planes[j] = tl[:, :, off:off + w]
-                gr = grouped_pool.tile([P, cols, PACK], BF16, name="group", align_bytes=64)
-                grouped[j] = gr
-                if INTERLEAVER[j] in "PQ":
-                    half = BANK // 2
-                    for c in range(0, cols, half):
-                        b = min([bb for bb in range(BANKS) if bb not in bank_of.values()], key=lambda bb: bank_age[bb])
-                        st = psum.tile([P, half * PACK], BF16, name="bank%d" % b)
-                        for q in range(2):
-                            cs = slice(c + q * P, c + (q + 1) * P)
-                            nc.tensor.matmul(out=st[:, q * BANK:(q + 1) * BANK].rearrange("p (c i t) -> p c t i", i=PE_RUN, t=PACK), lhsT=ident[:],
-                                             rhs=planes[j][:, :, cs].rearrange("p t (c i) -> p c t i", i=PE_RUN), start=True, stop=True)
-                        dst = gr[:, c:c + half, :].rearrange("p c t -> p (c t)")
-                        if INTERLEAVER[j] == "P":
-                            nc.scalar.copy(out=dst, in_=st[:])
-                        else:
-                            nc.vector.tensor_copy(out=dst, in_=st[:])
-                        tick += 1
-                        bank_age[b] = tick
-                else:
-                    dst = gr[:].rearrange("p (c i) t -> p c t i", i=RUN)
-                    src = planes[j].rearrange("p t (c i) -> p c t i", i=RUN)
-                    runs = cols // RUN
-                    cut = {"V": 0, "S": 0, "G": runs, "g": 3 * runs // 4, "h": 3 * runs // 4}[INTERLEAVER[j]]
-                    if cut > 0:
-                        nc.gpsimd.tensor_scalar(out=gr[:, 0:cut * RUN, :], in0=planes[j][:, :, 0:cut * RUN].rearrange("p t c -> p c t"),
-                                                scalar1=1.0, scalar2=0.0, op0=ALU.mult, op1=ALU.add)
-                    if cut < runs:
-                        if INTERLEAVER[j] in "Vh":
-                            nc.vector.tensor_copy(out=dst[:, cut:runs], in_=src[:, cut:runs])
-                        else:
-                            nc.scalar.copy(out=dst[:, cut:runs], in_=src[:, cut:runs])
-            elif op[0] == "quant":
-                j = op[1]
-                kind, c0, w, gs = CHUNKS[j]
-                cols = w * len(gs)
-                codes = keep.tile([P, cols], U32, name="codes%d" % j, align_bytes=64)
-                scales = keep.tile([P, cols], U8, name="scales%d" % j, align_bytes=64)
-                nc.vector.quantize_mx(out=codes[:].bitcast(FP8X4), scales=scales[:], in_=grouped[j][:].rearrange("p c t -> p (c t)"))
-                for gi, g in enumerate(gs):
-                    if kind == "D":
-                        for m in range(w // P):
-                            cs = slice(gi * w + m * P, gi * w + (m + 1) * P)
-                            operand[(c0 // P + m, g)] = (codes[:, cs], scales[:, cs])
+        planes, woven, quantised = {}, {}, {}
+        bank_of, sums = {}, {}
+        bank_queue = list(range(BANKS))
+
+        def prep(chunk):
+            operand, c0, width, passes = CHUNKS[chunk]
+            if operand == "h":
+                g = passes[0]
+                for t in range(PACK):
+                    row = loaded[("h", g, 0)][:, t, :]
+                    nc.vector.tensor_scalar(out=row, in0=row, scalar1=0.0, scalar2=gate_sb[:, g, t:t + 1],
+                                            op0=ALU.max, op1=ALU.mult)
+                return
+            plane = plane_pool.tile([P, PACK, width * len(passes)], BF16, name="plane", align_bytes=64)
+            planes[chunk] = plane[:]
+            for i, g in enumerate(passes):
+                for t in range(PACK):
+                    dst = plane[:, t, i * width:(i + 1) * width]
+                    src = loaded[(operand, g, c0)][:, t, 0:width]
+                    if chunk in WIDENED_BY_VECTOR:
+                        nc.vector.tensor_scalar(out=dst, in0=src.bitcast(FP8), scalar1=scale_sb[:, g, t:t + 1],
+                                                scalar2=None, op0=ALU.mult)
                     else:
-                        cs = slice(gi * w, (gi + 1) * w)
-                        operand[((kind, c0), g)] = (codes[:, cs], scales[:, cs])
-            elif op[0] == "mm":
-                grp, g = op[1], op[2]
-                if g == 0:
-                    free = [b for b in range(BANKS) if b not in bank_of.values()]
-                    b = min(free, key=lambda bb: bank_age[bb])
-                    bank_of[grp] = b
-                    acc_tile[grp] = psum.tile([P, BANK], F32, name="bank%d" % b)
-                lhs, lhs_scale = operand[(grp[0], g)]
-                rhs, rhs_scale = operand[(grp[1], g)]
-                nc.tensor.matmul_mx(out=acc_tile[grp][:], lhsT=lhs.bitcast(FP8X4), lhsT_scale=lhs_scale, rhs=rhs.bitcast(FP8X4), rhs_scale=rhs_scale,
-                                    start=(g == 0), stop=(g == PASSES - 1))
+                        nc.scalar.activation(out=dst, in_=src.bitcast(FP8), func=ACT.Copy, scale=scale_sb[:, g, t:t + 1])
+
+        def weave(chunk):
+            operand, c0, width, passes = CHUNKS[chunk]
+            cols = width * len(passes)
+            src = planes[chunk] if operand == "dy" else loaded[(operand, passes[0], c0)][:, :, 0:width]
+            dst = woven_pool.tile([P, cols, PACK], BF16, name="woven", align_bytes=64)
+            woven[chunk] = dst
+            if chunk in WOVEN_BY_TENSOR:
+                for c in range(0, cols, 2 * P):
+                    bank = bank_queue.pop(0)
+                    bank_queue.append(bank)
+                    staged = psum.tile([P, 2 * BANK], BF16, name="bank%d" % bank)
+                    for half in range(2):
+                        nc.tensor.matmul(
+                            out=staged[:, half * BANK:(half + 1) * BANK].rearrange("p (c i t) -> p c t i", i=MATMUL_RUN, t=PACK),
+                            lhsT=ident[:],
+                            rhs=src[:, :, c + half * P:c + (half + 1) * P].rearrange("p t (c i) -> p c t i", i=MATMUL_RUN),
+                            start=True, stop=True)
+                    nc.scalar.copy(out=dst[:, c:c + 2 * P, :].rearrange("p c t -> p (c t)"), in_=staged[:])
+                return
+            dst_runs = dst[:].rearrange("p (c i) t -> p c t i", i=COPY_RUN)
+            src_runs = src.rearrange("p t (c i) -> p c t i", i=COPY_RUN)
+            if chunk in WOVEN_BY_VECTOR:
+                nc.vector.tensor_copy(out=dst_runs, in_=src_runs)
             else:
-                grp = op[1]
-                m, (kind, c0) = grp
-                res = result_pool.tile([P, BANK], F32, name="res")
-                dst = (out_1 if kind == "X" else out_0)[m * P:(m + 1) * P, c0:c0 + BANK]
-                prior = accs[("V" if kind == "X" else "W", m, c0)]
-                if VIA_GPSIMD[n_added]:
-                    sums = grouped_pool.tile([P, BANK], F32, name="sums", bufs=2)
-                    nc.scalar.copy(out=sums[:], in_=acc_tile[grp][:])
-                    nc.gpsimd.tensor_tensor(out=res[:], in0=sums[:], in1=prior, op=ALU.add)
-                    nc.sync.dma_start(out=dst, in_=res[:])
-                else:
-                    pieces = 2 if n_added == len(VIA_GPSIMD) - 1 else 1
-                    for q in range(pieces):
-                        cs = slice(q * BANK // pieces, (q + 1) * BANK // pieces)
-                        nc.vector.tensor_tensor(out=res[:, cs], in0=acc_tile[grp][:, cs], in1=prior[:, cs], op=ALU.add)
-                        nc.sync.dma_start(out=dst[:, cs], in_=res[:, cs])
-                n_added += 1
-                tick += 1
-                bank_age[bank_of.pop(grp)] = tick
+                nc.scalar.copy(out=dst_runs, in_=src_runs)
+
+        def quant(chunk):
+            operand, c0, width, passes = CHUNKS[chunk]
+            codes = keep.tile([P, width * len(passes)], U32, name="codes_" + chunk, align_bytes=64)
+            scales = keep.tile([P, width * len(passes)], U8, name="scales_" + chunk, align_bytes=64)
+            nc.vector.quantize_mx(out=codes[:].bitcast(FP8X4), scales=scales[:],
+                                  in_=woven[chunk][:].rearrange("p c t -> p (c t)"))
+            span = P if operand == "dy" else width
+            for i, g in enumerate(passes):
+                for c in range(0, width, span):
+                    key = (c0 + c) // P if operand == "dy" else (operand, c0)
+                    cols = slice(i * width + c, i * width + c + span)
+                    quantised[(key, g)] = (codes[:, cols], scales[:, cols])
+
+        def mx_pass(tile, g):
+            if g == 0:
+                bank_of[tile] = bank_queue.pop(0)
+                sums[tile] = psum.tile([P, BANK], F32, name="bank%d" % bank_of[tile])
+            lhs, lhs_scale = quantised[(tile[0], g)]
+            rhs, rhs_scale = quantised[(tile[1], g)]
+            nc.tensor.matmul_mx(out=sums[tile][:], lhsT=lhs.bitcast(FP8X4), lhsT_scale=lhs_scale,
+                                rhs=rhs.bitcast(FP8X4), rhs_scale=rhs_scale, start=(g == 0), stop=(g == PASSES - 1))
+
+        def add(tile, is_last):
+            m, (operand, c0) = tile
+            dst = (out_1 if operand == "x" else out_0)[m * P:(m + 1) * P, c0:c0 + BANK]
+            acc = prior[("acc_v" if operand == "x" else "acc_w", m, c0)]
+            result = result_pool.tile([P, BANK], F32, name="result")
+            piece = BANK // 2 if is_last else BANK
+            for c in range(0, BANK, piece):
+                cols = slice(c, c + piece)
+                nc.vector.tensor_tensor(out=result[:, cols], in0=sums[tile][:, cols], in1=acc[:, cols], op=ALU.add)
+                nc.sync.dma_start(out=dst[:, cols], in_=result[:, cols])
+            bank_queue.append(bank_of[tile])
+
+        run = {"prep": prep, "weave": weave, "quant": quant, "pass": mx_pass, "add": add}
+        for step in program():
+            run[step[0]](*step[1:])

from contextlib import ExitStack

import concourse.mybir as mybir
from concourse.masks import make_identity

T, N, K, D = 2048, 1024, 1024, 512
FLOPS = 2 * T * N * (K + D)

F32 = mybir.dt.float32
BF16 = mybir.dt.bfloat16
U32 = mybir.dt.uint32
U8 = mybir.dt.uint8
FP8 = mybir.dt.float8_e4m3fn
FP8X4 = mybir.dt.float8_e4m3fn_x4
ALU = mybir.AluOpType
ACT = mybir.ActivationFunctionType

P = 128
PACK = 4
PASSES = T // (P * PACK)
BANK = 512
BANKS = 8
GROUPS = (N // P) * ((K + D) // BANK)
ACC_ROWS = 4
COPY_RUN = 4
MATMUL_RUN = 8
PLANE_BUFS = 7
WOVEN_BUFS = 5

CHUNKS = {
    "x0": ("x", 0, 512, [0]), "dyA0": ("dy", 0, 512, [0]),
    "x1": ("x", 0, 512, [1]), "dyA1": ("dy", 0, 512, [1]),
    "x2": ("x", 0, 512, [2]), "dyA2": ("dy", 0, 512, [2]),
    "x3": ("x", 0, 512, [3]), "dyA3": ("dy", 0, 512, [3]),
    "aA0": ("h", 0, 512, [0]), "aA1": ("h", 0, 512, [1]), "aA2": ("h", 0, 512, [2]), "aA3": ("h", 0, 512, [3]),
    "dyB0": ("dy", 512, 256, [0, 1]), "dyB1": ("dy", 512, 256, [2, 3]),
    "aB0": ("h", 512, 512, [0]), "aB1": ("h", 512, 512, [1]), "aB2": ("h", 512, 512, [2]), "aB3": ("h", 512, 512, [3]),
    "dyC": ("dy", 768, 128, [0, 1, 2, 3]),
    "dyD0": ("dy", 896, 128, [0, 1]), "dyD1": ("dy", 896, 128, [2, 3]),
}

WOVEN_BY_VECTOR = ["x0", "dyA0", "x1", "dyA2", "aA1", "aA2", "aB3"]
WOVEN_BY_TENSOR = ["dyA1", "x2", "dyA3", "aA0", "dyB0"]
WIDENED_BY_VECTOR = ["dyA0", "dyA1"]

LOADS = [
    ("dy", 0, 0, 512), ("dy", 3, 0, 1024), ("dy", 1, 0, 1024), ("dy", 2, 0, 1024),
    ("x", 1, 0, 512), ("x", 0, 0, 512), ("x", 3, 0, 512), ("x", 2, 0, 512),
    ("dy", 0, 512, 512), ("h", 0, 0, 1024), ("h", 3, 0, 1024), ("h", 1, 0, 1024),
    ("h", 2, 0, 1024), ("acc_v", 0, 0, 512), ("acc_w", 0, 0, 1024), ("acc_v", 1, 0, 512),
    ("acc_w", 1, 0, 1024),
]

ORDER = """
prep:dyA3 prep:dyA0 prep:dyA1 weave:dyA0 prep:dyA2 prep:dyB1 weave:x1 weave:x0 weave:dyA2 quant:dyA0
quant:dyA2 quant:x0 weave:dyA3 weave:dyA1 quant:dyA1 weave:x3 weave:x2 prep:dyB0 mm:x0 quant:dyA3
mm:dyA0 quant:x1 prep:aA0 quant:x3 mm:x1 prep:aA3 quant:x2 mm:dyA1 prep:aA1 prep:aA2 weave:aA0 mm:x2
weave:aA1 weave:aA3 weave:dyB0 mm:dyA2 quant:aA0 mm:x3 mm:dyA3 weave:aA2 quant:aA1 weave:dyB1
quant:aA2 mm:aA0 mm:aA1 add quant:aA3 add quant:dyB0 weave:aB0 weave:aB2 quant:dyB1 add mm:aA2 add
mm:aA3 add mm:dyB0 weave:aB1 mm:dyB1 prep:dyC quant:aB0 add add add add add mm:aB0 quant:aB1 mm:aB1
quant:aB2 weave:aB3 quant:aB3 weave:dyC add prep:dyD0 mm:aB2 add quant:dyC mm:aB3 prep:dyD1 add add
weave:dyD0 weave:dyD1 add add add mm:dyC quant:dyD0 add add quant:dyD1 mm:dyD0 mm:dyD1 add add add
add add
"""


def program():
    steps, ready, tiles, next_pass, finished = [], set(), [], {}, []
    row_tiles, moving = [], []
    added = 0
    for token in ORDER.split():
        if token == "add":
            steps.append(("add", finished[added], added == GROUPS - 1))
            added += 1
            continue
        step, chunk = token.split(":")
        if step != "mm":
            steps.append((step, chunk))
            continue
        operand, c0, width, passes = CHUNKS[chunk]
        keys = list(range(c0 // P, (c0 + width) // P)) if operand == "dy" else [(operand, c0)]
        for key in keys:
            for g in passes:
                ready.add((key, g))
        if passes[0] == 0:
            if operand == "dy":
                tiles.extend([(m, n) for m in keys for n in moving])
                row_tiles.extend(keys)
            else:
                tiles.extend([(m, keys[0]) for m in row_tiles])
                moving.extend(keys)
        for tile in tiles:
            g = next_pass.get(tile, 0)
            while g < PASSES and (tile[0], g) in ready and (tile[1], g) in ready:
                steps.append(("pass", tile, g))
                g += 1
                if g == PASSES:
                    finished.append(tile)
            next_pass[tile] = g
    return steps


def tile_gated_skip_wgrad_fp8_d3_kernel(tc, dy_bytes, dy_scale, h, gate, x, acc_w, acc_v, out_0, out_1):
    nc = tc.nc
    with ExitStack() as ctx:
        keep = ctx.enter_context(tc.tile_pool(name="keep", bufs=1))
        plane_pool = ctx.enter_context(tc.tile_pool(name="planes", bufs=PLANE_BUFS))
        woven_pool = ctx.enter_context(tc.tile_pool(name="woven", bufs=WOVEN_BUFS))
        result_pool = ctx.enter_context(tc.tile_pool(name="result", bufs=GROUPS))
        psum = ctx.enter_context(tc.psum_pool(name="psum", bufs=1))
        ctx.enter_context(tc.manual_schedule())

        scale_sb = keep.tile([P, PASSES, PACK], F32, name="scale_sb")
        gate_sb = keep.tile([P, PASSES, PACK], BF16, name="gate_sb")
        nc.scalar.dma_start(out=scale_sb[:], in_=dy_scale.rearrange("(g p t) o -> p g (t o)", p=P, t=PACK))
        nc.scalar.dma_start(out=gate_sb[:], in_=gate.rearrange("(g p t) o -> p g (t o)", p=P, t=PACK))

        ident_f32 = keep.tile([P, P], F32, name="ident_f32")
        ident = keep.tile([P, P], BF16, name="ident")
        make_identity(nc, ident_f32[:])
        nc.scalar.activation(out=ident[:], in_=ident_f32[:], func=ACT.Copy)

        loaded, prior = {}, {}
        for tensor, index, c0, width in LOADS:
            label = "%s_in_%d_%d" % (tensor, index, c0)
            if tensor in ("acc_w", "acc_v"):
                rows = (acc_w if tensor == "acc_w" else acc_v).rearrange("(m p) c -> p m c", p=P)
                m0 = index * ACC_ROWS
                dst = keep.tile([P, ACC_ROWS, width], BF16, name=label, align_bytes=64)
                nc.sync.dma_start(out=dst[:], in_=rows[:, m0:m0 + ACC_ROWS, c0:c0 + width])
                for m in range(ACC_ROWS):
                    for c in range(0, width, BANK):
                        prior[(tensor, m0 + m, c0 + c)] = dst[:, m, c:c + BANK]
            else:
                rows = {"dy": dy_bytes, "h": h, "x": x}[tensor].rearrange("(g p t) c -> g p t c", p=P, t=PACK)
                dst = keep.tile([P, PACK, width], U8 if tensor == "dy" else BF16, name=label, align_bytes=64)
                nc.sync.dma_start(out=dst[:], in_=rows[index][:, :, c0:c0 + width])
                for c in range(0, width, P):
                    loaded[(tensor, index, c0 + c)] = dst[:, :, c:width]

        planes, woven, quantised = {}, {}, {}
        bank_of, sums = {}, {}
        bank_queue = list(range(BANKS))

        def prep(chunk):
            operand, c0, width, passes = CHUNKS[chunk]
            if operand == "h":
                g = passes[0]
                for t in range(PACK):
                    row = loaded[("h", g, 0)][:, t, :]
                    nc.vector.tensor_scalar(out=row, in0=row, scalar1=0.0, scalar2=gate_sb[:, g, t:t + 1],
                                            op0=ALU.max, op1=ALU.mult)
                return
            plane = plane_pool.tile([P, PACK, width * len(passes)], BF16, name="plane", align_bytes=64)
            planes[chunk] = plane[:]
            for i, g in enumerate(passes):
                for t in range(PACK):
                    dst = plane[:, t, i * width:(i + 1) * width]
                    src = loaded[(operand, g, c0)][:, t, 0:width]
                    if chunk in WIDENED_BY_VECTOR:
                        nc.vector.tensor_scalar(out=dst, in0=src.bitcast(FP8), scalar1=scale_sb[:, g, t:t + 1],
                                                scalar2=None, op0=ALU.mult)
                    else:
                        nc.scalar.activation(out=dst, in_=src.bitcast(FP8), func=ACT.Copy, scale=scale_sb[:, g, t:t + 1])

        def weave(chunk):
            operand, c0, width, passes = CHUNKS[chunk]
            cols = width * len(passes)
            src = planes[chunk] if operand == "dy" else loaded[(operand, passes[0], c0)][:, :, 0:width]
            dst = woven_pool.tile([P, cols, PACK], BF16, name="woven", align_bytes=64)
            woven[chunk] = dst
            if chunk in WOVEN_BY_TENSOR:
                for c in range(0, cols, 2 * P):
                    bank = bank_queue.pop(0)
                    bank_queue.append(bank)
                    staged = psum.tile([P, 2 * BANK], BF16, name="bank%d" % bank)
                    for half in range(2):
                        nc.tensor.matmul(
                            out=staged[:, half * BANK:(half + 1) * BANK].rearrange("p (c i t) -> p c t i", i=MATMUL_RUN, t=PACK),
                            lhsT=ident[:],
                            rhs=src[:, :, c + half * P:c + (half + 1) * P].rearrange("p t (c i) -> p c t i", i=MATMUL_RUN),
                            start=True, stop=True)
                    nc.scalar.copy(out=dst[:, c:c + 2 * P, :].rearrange("p c t -> p (c t)"), in_=staged[:])
                return
            dst_runs = dst[:].rearrange("p (c i) t -> p c t i", i=COPY_RUN)
            src_runs = src.rearrange("p t (c i) -> p c t i", i=COPY_RUN)
            if chunk in WOVEN_BY_VECTOR:
                nc.vector.tensor_copy(out=dst_runs, in_=src_runs)
            else:
                nc.scalar.copy(out=dst_runs, in_=src_runs)

        def quant(chunk):
            operand, c0, width, passes = CHUNKS[chunk]
            codes = keep.tile([P, width * len(passes)], U32, name="codes_" + chunk, align_bytes=64)
            scales = keep.tile([P, width * len(passes)], U8, name="scales_" + chunk, align_bytes=64)
            nc.vector.quantize_mx(out=codes[:].bitcast(FP8X4), scales=scales[:],
                                  in_=woven[chunk][:].rearrange("p c t -> p (c t)"))
            span = P if operand == "dy" else width
            for i, g in enumerate(passes):
                for c in range(0, width, span):
                    key = (c0 + c) // P if operand == "dy" else (operand, c0)
                    cols = slice(i * width + c, i * width + c + span)
                    quantised[(key, g)] = (codes[:, cols], scales[:, cols])

        def mx_pass(tile, g):
            if g == 0:
                bank_of[tile] = bank_queue.pop(0)
                sums[tile] = psum.tile([P, BANK], F32, name="bank%d" % bank_of[tile])
            lhs, lhs_scale = quantised[(tile[0], g)]
            rhs, rhs_scale = quantised[(tile[1], g)]
            nc.tensor.matmul_mx(out=sums[tile][:], lhsT=lhs.bitcast(FP8X4), lhsT_scale=lhs_scale,
                                rhs=rhs.bitcast(FP8X4), rhs_scale=rhs_scale, start=(g == 0), stop=(g == PASSES - 1))

        def add(tile, is_last):
            m, (operand, c0) = tile
            dst = (out_1 if operand == "x" else out_0)[m * P:(m + 1) * P, c0:c0 + BANK]
            acc = prior[("acc_v" if operand == "x" else "acc_w", m, c0)]
            result = result_pool.tile([P, BANK], F32, name="result")
            piece = BANK // 2 if is_last else BANK
            for c in range(0, BANK, piece):
                cols = slice(c, c + piece)
                nc.vector.tensor_tensor(out=result[:, cols], in0=sums[tile][:, cols], in1=acc[:, cols], op=ALU.add)
                nc.sync.dma_start(out=dst[:, cols], in_=result[:, cols])
            bank_queue.append(bank_of[tile])

        run = {"prep": prep, "weave": weave, "quant": quant, "pass": mx_pass, "add": add}
        for step in program():
            run[step[0]](*step[1:])
